import numpy as np
import ml_dtypes


def mxq(x, axis, fmt="e4m3"):
    dtype, down = {"e4m3": (ml_dtypes.float8_e4m3fn, 7), "e5m2": (ml_dtypes.float8_e5m2, 14)}[fmt]
    v = np.moveaxis(np.asarray(x, np.float32).astype(ml_dtypes.bfloat16).astype(np.float64), axis, -1)
    blocks = v.reshape(v.shape[:-1] + (-1, 32))
    amax = np.abs(blocks).max(-1, keepdims=True)
    byte = np.maximum(np.where(amax > 0, np.frexp(amax)[1] - 1 + 127, 0) - down, 1)
    scale = np.exp2(byte - 127.0)
    codes = (blocks / scale).astype(np.float32).astype(dtype).astype(np.float64)
    return np.moveaxis((codes * scale).reshape(v.shape), -1, axis)


WIDE = False


def mx_kscale(k):
    if not WIDE:
        return np.ones(k)
    levels = np.array([10, -10, 5, -5, 0])
    if k % 512:
        return np.exp2(np.random.permutation(np.resize(levels, k // 32))).repeat(32)
    a = np.empty((k // 512, 16))
    for p in range(k // 512):
        a[p, :8] = np.random.permutation(np.resize(levels, 8))
        for g in range(8):
            far = levels[np.abs(levels - a[p, g]) >= 10]
            a[p, g + 8] = far[np.random.randint(len(far))]
    return np.exp2(a.ravel()).repeat(32)


def f64(x):
    return np.asarray(x).astype(np.float64)


def striped(idx):
    return np.tile(idx.reshape(-1, 16).T, (8, 1)).astype(np.uint16)


def unstriped(offs):
    return offs[:16].T.reshape(-1).astype(np.int64)


E2M1 = np.array([0.0, 0.5, 1.0, 1.5, 2.0, 3.0, 4.0, 6.0, -0.0, -0.5, -1.0, -1.5, -2.0, -3.0, -4.0, -6.0])


def pack_weight(w, fmt):
    k, n = w.shape
    w = f64(np.asarray(w, np.float32).astype(ml_dtypes.bfloat16)).reshape(k // 32, 32, n)
    amax = np.abs(w).max(1)
    if fmt == "e4m3":
        byte = np.frexp(amax)[1] - 1 + 127 - 7
    else:
        mant, ex = np.frexp(amax / 6.0)
        byte = np.where(mant > 0.5, ex, ex - 1) + 127
    byte = np.clip(np.where(amax > 0, byte, 1), 1, 254)
    scaled = (w * np.exp2(127.0 - byte)[:, None, :]).reshape(k, n).astype(np.float32)
    by_word = np.ascontiguousarray(scaled.reshape(k // 512, 128, 4, n).transpose(0, 1, 3, 2))
    if fmt == "e4m3":
        words = by_word.astype(ml_dtypes.float8_e4m3fn).view(np.uint8)
    else:
        c = by_word.astype(ml_dtypes.float4_e2m1fn).view(np.uint8) & 0xF
        words = (c[..., 0::2] | (c[..., 1::2] << 4)).reshape(k // 512, 128, 2 * n)
    return np.ascontiguousarray(words), np.ascontiguousarray(byte.astype(np.uint8).reshape(k // 512, 16, n))


def unpack_weight(words, scales, fmt):
    g, _, n = scales.shape
    words = np.ascontiguousarray(words).reshape(g, 128, n, -1)
    if fmt == "e4m3":
        vals = words.view(ml_dtypes.float8_e4m3fn).astype(np.float64)
    else:
        nib = np.empty((g, 128, n, 4), np.uint8)
        nib[..., 0::2] = words & 0xF
        nib[..., 1::2] = words >> 4
        vals = E2M1[nib]
    vals = vals * np.repeat(np.exp2(scales.astype(np.float64) - 127.0), 8, axis=1)[..., None]
    return vals.transpose(0, 1, 3, 2).reshape(g * 512, n)


def gelu(v):
    return 0.5 * v * (1.0 + np.tanh(np.sqrt(2.0 / np.pi) * (v + 0.044715 * v**3)))


K, H, N, T, S, T2 = 1024, 512, 768, 2048, 1024, 2048

def setup_inputs():
    n = np.random.standard_normal
    s = mx_kscale(K)[:, None]
    u = mx_kscale(H)[:, None]
    tab_words, tab_scales = pack_weight(n((K, T)) * s, "e4m3")
    w4_words, w4_scales = pack_weight(1.2 * n((K, H)) / np.sqrt(K) / s, "e2m1")
    return {
        "tab_words": tab_words, "tab_scales": tab_scales,
        "offs": striped(np.random.permutation(T)[:S]),
        "offs2": striped(np.random.permutation(T)[:S]),
        "offs3": striped(np.random.permutation(T2)[:S]),
        "w4_words": w4_words, "w4_scales": w4_scales,
        "wb": (0.5 * n((K, H)) / np.sqrt(K) / s).astype(np.float32),
        "weekday": np.exp(0.4 * n((H, S))).astype(np.float32),
        "gain": (np.exp(0.3 * n(H)) * u[:, 0]).astype(np.float32),
        "wc": (2.5 * n((H, N)) / np.sqrt(H) / u).astype(np.float32),
        "rank": np.exp(0.4 * n(N)).astype(np.float32),
        "wgo": np.exp(0.3 * n((128, S))).astype(np.float32),
    }

def reference(tab_words, tab_scales, offs, offs2, offs3, w4_words, w4_scales, wb, weekday, gain, wc, rank, wgo):
    TW = unpack_weight(tab_words, tab_scales, "e4m3")
    v = TW[:, unstriped(offs)]
    v2 = TW[:, unstriped(offs2)]
    w4 = unpack_weight(w4_words, w4_scales, "e2m1")
    ra = np.tanh(f64(weekday) * (w4.T @ v))
    db = np.sin(mxq(f64(wb), 0, "e4m3").T @ v2)
    z = f64(gain)[:, None] * (ra * db)
    y = mxq(f64(wc), 0, "e4m3").T @ mxq(z, 0, "e4m3")
    y = f64(rank)[:, None] * y
    out = np.zeros((N, T2))
    out[:, unstriped(offs3)] = np.tile(f64(wgo), (N // 128, 1)) * y
    return out

@@ -1,0 +1,291 @@
+from contextlib import ExitStack
+
+import concourse.mybir as mybir
+
+K, H, N, T, S = 1024, 512, 768, 2048, 1024
+FLOPS = 2 * K * H * S * 2 + 2 * H * N * S
+
+F32 = mybir.dt.float32
+BF16 = mybir.dt.bfloat16
+I32 = mybir.dt.int32
+U32 = mybir.dt.uint32
+U16 = mybir.dt.uint16
+U8 = mybir.dt.uint8
+FP8X4 = mybir.dt.float8_e4m3fn_x4
+FP4X4 = mybir.dt.float4_e2m1fn_x4
+MULT = mybir.AluOpType.mult
+ACT = mybir.ActivationFunctionType
+
+P = 128
+PACK = 4
+PASSES = K // (P * PACK)
+QUADS = 4
+CHUNK = 512
+CHUNKS = S // CHUNK
+ROW_TILES = N // P
+PAGES = 3
+WC_PIECE = 256
+
+
+def tile_list_carpool_pair_cards_kernel(
+    tc, tab_words, tab_scales, offs, offs2, offs3, w4_words, w4_scales, wb, weekday, gain, wc, rank, wgo, out
+):
+    nc = tc.nc
+    with ExitStack() as ctx:
+        keep = ctx.enter_context(tc.tile_pool(name="keep", bufs=1))
+        ring = ctx.enter_context(tc.tile_pool(name="ring", bufs=4))
+        psum = ctx.enter_context(tc.psum_pool(name="psum", bufs=8))
+
+        def held(shape, dtype, name):
+            return keep.tile(shape, dtype, name=name, align_bytes=64)
+
+        def entries(c):
+            return slice(c * CHUNK, (c + 1) * CHUNK)
+
+        def list_columns(c):
+            return slice(c * CHUNK // 16, (c + 1) * CHUNK // 16)
+
+        riders = held([P, S // 16], U16, "riders")
+        drivers = held([P, S // 16], U16, "drivers")
+        cards = held([P, S // 16], U16, "cards")
+        tab_planes = held([P, T], U8, "tab_planes")
+        tab = [held([P, T], U32, "tab%d" % a) for a in range(PASSES)]
+        w4_raw = held([P, PASSES, H], U16, "w4_raw")
+        w4_raw_planes = held([P, PASSES, H], U8, "w4_raw_planes")
+        rider_plane1 = held([P, S], U8, "rider_plane1")
+        wb_raw = [held([P, PACK, H], F32, "wb_raw%d" % a) for a in range(PASSES)]
+        day = [held([P, PACK, CHUNK], F32, "day%d" % c) for c in range(CHUNKS)]
+        wc_raw = [held([P, PACK, WC_PIECE], F32, "wc_raw%d" % i) for i in range(N // WC_PIECE)]
+        gains = held([P, PACK], F32, "gains")
+        ranks = held([P, ROW_TILES], F32, "ranks")
+        go = held([P, S], F32, "go")
+        pages = [held([P, T], F32, "page%d" % i) for i in range(PAGES)]
+
+        nc.vector.memset(tab_planes[:].bitcast(I32), 0)
+        nc.vector.memset(w4_raw_planes[:].rearrange("p a c -> p (a c)").bitcast(I32), 0)
+        nc.vector.memset(rider_plane1[:].bitcast(I32), 0)
+        for page in pages:
+            nc.vector.memset(page[:].bitcast(I32), 0)
+
+        def load_tab(a):
+            nc.sync.dma_start(out=tab[a][:].bitcast(I32), in_=tab_words[a].rearrange("p t i -> p (t i)").bitcast(I32))
+
+        def load_wb(a):
+            nc.sync.dma_start(out=wb_raw[a][:], in_=wb[a * 512 : (a + 1) * 512, :].rearrange("(p j) c -> p j c", j=PACK))
+
+        nc.sync.dma_start(riders[:], offs)
+        nc.sync.dma_start(out=w4_raw[:].bitcast(I32), in_=w4_words.bitcast(I32).rearrange("a p c -> p a c"))
+        scales_i32 = tab_scales.bitcast(I32)
+        for q in range(QUADS):
+            nc.sync.dma_start(
+                out=tab_planes[32 * q : 32 * q + 4 * PASSES, :].bitcast(I32), in_=scales_i32[:, 4 * q : 4 * q + 4, :]
+            )
+        nc.sync.dma_start(drivers[:], offs2)
+        load_tab(0)
+        w4_scales_i32 = w4_scales.bitcast(I32)
+        for q in range(QUADS):
+            nc.sync.dma_start(
+                out=w4_raw_planes[32 * q : 32 * q + 4, :, :].bitcast(I32),
+                in_=w4_scales_i32[:, 4 * q : 4 * q + 4, :].rearrange("a r c -> r a c"),
+            )
+        load_wb(0)
+        load_tab(1)
+        load_wb(1)
+        day_rows = weekday.rearrange("(p t) j -> p t j", t=PACK)
+        wc_rows = wc.rearrange("(p t) n -> p t n", t=PACK)
+        nc.sync.dma_start(out=day[0][:], in_=day_rows[:, :, entries(0)])
+        nc.sync.dma_start(out=gains[:], in_=gain.rearrange("(p t) -> p t", t=PACK))
+        nc.sync.dma_start(out=wc_raw[0][:], in_=wc_rows[:, :, 0:WC_PIECE])
+        nc.sync.dma_start(out=day[1][:], in_=day_rows[:, :, entries(1)])
+        nc.sync.dma_start(cards[:], offs3)
+        with nc.allow_non_contiguous_dma("one rank value to a partition and row tile"):
+            nc.sync.dma_start(out=ranks[:], in_=rank.rearrange("(u p) -> p u", p=P))
+        nc.sync.dma_start(out=go[:], in_=wgo)
+        for i in range(1, N // WC_PIECE):
+            nc.sync.dma_start(out=wc_raw[i][:], in_=wc_rows[:, :, i * WC_PIECE : (i + 1) * WC_PIECE])
+
+        rider_planes = held([P, S], U8, "rider_planes")
+        driver_planes = held([P, S], U8, "driver_planes")
+        nc.vector.tensor_copy(rider_planes[:], tab_planes[:].indirect(riders[:]))
+        for q in range(QUADS):
+            nc.scalar.dma_start(
+                out=rider_plane1[32 * q : 32 * q + 4, :].bitcast(I32),
+                in_=rider_planes[32 * q + 4 : 32 * q + 8, :].bitcast(I32),
+            )
+        nc.vector.tensor_copy(driver_planes[:], tab_planes[:].indirect(drivers[:]))
+
+        w4 = held([P, PASSES, PACK, P], U16, "w4")
+        w4_planes = held([P, PASSES, PACK, P], U8, "w4_planes")
+        nc.vector.tensor_copy(w4[:], w4_raw[:].rearrange("p a (m t) -> p a t m", t=PACK))
+        nc.vector.tensor_copy(w4_planes[:], w4_raw_planes[:].rearrange("p a (m t) -> p a t m", t=PACK))
+
+        rider_words, driver_words = {}, {}
+
+        def gather_words(c, a):
+            rider_words[c, a] = held([P, CHUNK], U32, "rider_words%d%d" % (c, a))
+            driver_words[c, a] = held([P, CHUNK], U32, "driver_words%d%d" % (c, a))
+            nc.vector.tensor_copy(rider_words[c, a][:], tab[a][:].indirect(riders[:, list_columns(c)]))
+            nc.vector.tensor_copy(driver_words[c, a][:], tab[a][:].indirect(drivers[:, list_columns(c)]))
+
+        wb_rounded, wb_codes, wb_planes = {}, {}, {}
+
+        def round_wb(a):
+            wb_rounded[a] = held([P, PACK, P, PACK], BF16, "wb_rounded%d" % a)
+            nc.scalar.copy(
+                wb_rounded[a][:].rearrange("p t m j -> p m j t"),
+                wb_raw[a][:].rearrange("p j (m t) -> p m j t", t=PACK),
+            )
+
+        def quantise_wb(a):
+            wb_codes[a] = held([P, H], U32, "wb_codes%d" % a)
+            wb_planes[a] = held([P, H], U8, "wb_planes%d" % a)
+            nc.vector.quantize_mx(
+                out=wb_codes[a][:].bitcast(FP8X4),
+                scales=wb_planes[a][:],
+                in_=wb_rounded[a][:].rearrange("p t m j -> p (t m j)"),
+            )
+
+        wc_rounded, wc_codes, wc_planes = {}, {}, {}
+
+        def round_wc(i):
+            wc_rounded[i] = held([P, WC_PIECE, PACK], BF16, "wc_rounded%d" % i)
+            nc.scalar.copy(
+                wc_rounded[i][:].rearrange("p (n i) t -> p n t i", i=4),
+                wc_raw[i][:].rearrange("p t (n i) -> p n t i", i=4),
+            )
+
+        def quantise_wc(i):
+            wc_codes[i] = held([P, WC_PIECE], U32, "wc_codes%d" % i)
+            wc_planes[i] = held([P, WC_PIECE], U8, "wc_planes%d" % i)
+            nc.vector.quantize_mx(
+                out=wc_codes[i][:].bitcast(FP8X4),
+                scales=wc_planes[i][:],
+                in_=wc_rounded[i][:].rearrange("p n t -> p (n t)"),
+            )
+
+        rider_sums, ra, db, z, z_rounded, z_codes, z_planes = {}, {}, {}, {}, {}, {}, {}
+
+        def rider_products(c):
+            for t in range(PACK):
+                rider_sums[c, t] = psum.tile([P, CHUNK], F32, name="bank")
+                for a in range(PASSES):
+                    plane = rider_planes if a == 0 else rider_plane1
+                    nc.tensor.matmul_mx(
+                        out=rider_sums[c, t][:],
+                        lhsT=w4[:, a, t, :].bitcast(FP4X4),
+                        lhsT_scale=w4_planes[:, a, t, :],
+                        rhs=rider_words[c, a][:].bitcast(FP8X4),
+                        rhs_scale=plane[:, entries(c)],
+                        start=(a == 0),
+                        stop=(a == PASSES - 1),
+                    )
+
+        def driver_features(c):
+            for t in range(PACK):
+                bank = psum.tile([P, CHUNK], F32, name="bank")
+                columns = slice(t * P, (t + 1) * P)
+                for a in range(PASSES):
+                    nc.tensor.matmul_mx(
+                        out=bank[:],
+                        lhsT=wb_codes[a][:, columns].bitcast(FP8X4),
+                        lhsT_scale=wb_planes[a][:, columns],
+                        rhs=driver_words[c, a][:].bitcast(FP8X4),
+                        rhs_scale=driver_planes[4 * a :, entries(c)],
+                        start=(a == 0),
+                        stop=(a == PASSES - 1),
+                    )
+                db[c, t] = held([P, CHUNK], F32, "db%d%d" % (c, t))
+                nc.scalar.activation(db[c, t][:], bank[:], ACT.Sin)
+
+        def rider_features(c):
+            for t in range(PACK):
+                weighted = ring.tile([P, CHUNK], F32, name="weighted")
+                nc.vector.tensor_tensor(weighted[:], rider_sums[c, t][:], day[c][:, t, :], MULT)
+                ra[c, t] = held([P, CHUNK], F32, "ra%d%d" % (c, t))
+                nc.scalar.activation(ra[c, t][:], weighted[:], ACT.Tanh)
+
+        def pair_features(c):
+            z[c] = held([P, PACK, CHUNK], F32, "z%d" % c)
+            for t in range(PACK):
+                nc.vector.scalar_tensor_tensor(z[c][:, t, :], ra[c, t][:], gains[:, t : t + 1], db[c, t][:], MULT, MULT)
+            z_rounded[c] = held([P, CHUNK, PACK], BF16, "z_rounded%d" % c)
+            nc.scalar.copy(
+                z_rounded[c][:].rearrange("p (j i) t -> p j t i", i=4),
+                z[c][:].rearrange("p t (j i) -> p j t i", i=4),
+            )
+
+        def quantise_z(c):
+            z_codes[c] = held([P, CHUNK], U32, "z_codes%d" % c)
+            z_planes[c] = held([P, CHUNK], U8, "z_planes%d" % c)
+            nc.vector.quantize_mx(
+                out=z_codes[c][:].bitcast(FP8X4),
+                scales=z_planes[c][:],
+                in_=z_rounded[c][:].rearrange("p j t -> p (j t)"),
+            )
+
+        y = [held([P, S], F32, "y%d" % u) for u in range(ROW_TILES)]
+
+        def card_values(u, c):
+            piece, first = divmod(u * P, WC_PIECE)
+            columns = slice(first, first + P)
+            bank = psum.tile([P, CHUNK], F32, name="bank")
+            nc.tensor.matmul_mx(
+                out=bank[:],
+                lhsT=wc_codes[piece][:, columns].bitcast(FP8X4),
+                lhsT_scale=wc_planes[piece][:, columns],
+                rhs=z_codes[c][:].bitcast(FP8X4),
+                rhs_scale=z_planes[c][:],
+                start=True,
+                stop=True,
+            )
+            nc.scalar.activation(y[u][:, entries(c)], bank[:], ACT.Copy, scale=ranks[:, u : u + 1])
+
+        def place_chunk(u, c):
+            nc.vector.tensor_tensor(
+                pages[u % PAGES][:].indirect(cards[:, list_columns(c)]), y[u][:, entries(c)], go[:, entries(c)], MULT
+            )
+
+        def place_all(u):
+            nc.vector.tensor_tensor(pages[u % PAGES][:].indirect(cards[:]), y[u][:], go[:], MULT)
+
+        def store(u):
+            nc.sync.dma_start(out=out[u * P : (u + 1) * P, :], in_=pages[u % PAGES][:])
+
+        for a in range(PASSES):
+            gather_words(0, a)
+        rider_products(0)
+        for a in range(PASSES):
+            round_wb(a)
+            gather_words(1, a)
+            quantise_wb(a)
+        driver_features(0)
+        rider_features(0)
+        round_wc(0)
+        pair_features(0)
+        rider_products(1)
+        driver_features(1)
+        rider_features(1)
+        quantise_wc(0)
+        quantise_z(0)
+        card_values(0, 0)
+        place_chunk(0, 0)
+        pair_features(1)
+        card_values(1, 0)
+        place_chunk(1, 0)
+        round_wc(1)
+        quantise_wc(1)
+        quantise_z(1)
+        card_values(2, 0)
+        place_chunk(2, 0)
+        for u in range(PAGES):
+            card_values(u, 1)
+            place_chunk(u, 1)
+            store(u)
+            if u == 0:
+                round_wc(2)
+                quantise_wc(2)
+        for u in range(PAGES, ROW_TILES):
+            for c in range(CHUNKS):
+                card_values(u, c)
+            place_all(u)
+            store(u)

@@ -36,8 +36,8 @@ def tile_list_carpool_pair_cards_kernel(
         ring = ctx.enter_context(tc.tile_pool(name="ring", bufs=4))
         psum = ctx.enter_context(tc.psum_pool(name="psum", bufs=8))
 
-        def held(shape, dtype, name):
-            return keep.tile(shape, dtype, name=name, align_bytes=64)
+        def held(shape, dtype, name, after=None):
+            return keep.tile(shape, dtype, name=name, tag=after or name, align_bytes=64)
 
         def entries(c):
             return slice(c * CHUNK, (c + 1) * CHUNK)
@@ -50,22 +50,23 @@ def tile_list_carpool_pair_cards_kernel(
         cards = held([P, S // 16], U16, "cards")
         tab_planes = held([P, T], U8, "tab_planes")
         tab = [held([P, T], U32, "tab%d" % a) for a in range(PASSES)]
-        w4_raw = held([P, PASSES, H], U16, "w4_raw")
-        w4_raw_planes = held([P, PASSES, H], U8, "w4_raw_planes")
+        w4_raw = held([P, PASSES, H // 2], I32, "w4_raw")
+        w4_raw_planes = held([P, PASSES, H // 4], I32, "w4_raw_planes")
         rider_plane1 = held([P, S], U8, "rider_plane1")
         wb_raw = [held([P, PACK, H], F32, "wb_raw%d" % a) for a in range(PASSES)]
         day = [held([P, PACK, CHUNK], F32, "day%d" % c) for c in range(CHUNKS)]
-        wc_raw = [held([P, PACK, WC_PIECE], F32, "wc_raw%d" % i) for i in range(N // WC_PIECE)]
-        gains = held([P, PACK], F32, "gains")
+        wc_raw = held([P, PACK, N], F32, "wc_raw")
+        gains = [held([P, 1], F32, "gain%d" % t) for t in range(PACK)]
         ranks = held([P, ROW_TILES], F32, "ranks")
         go = held([P, S], F32, "go")
-        pages = [held([P, T], F32, "page%d" % i) for i in range(PAGES)]
 
         nc.vector.memset(tab_planes[:].bitcast(I32), 0)
-        nc.vector.memset(w4_raw_planes[:].rearrange("p a c -> p (a c)").bitcast(I32), 0)
+        nc.vector.memset(w4_raw_planes[:], 0)
         nc.vector.memset(rider_plane1[:].bitcast(I32), 0)
-        for page in pages:
-            nc.vector.memset(page[:].bitcast(I32), 0)
+        warm_in = held([P, 1], F32, "warm_in")
+        warm_out = held([P, 1], F32, "warm_out")
+        nc.gpsimd.memset(warm_in[:], 0.0)
+        nc.scalar.activation(warm_out[:], warm_in[:], ACT.Silu)
 
         def load_tab(a):
             nc.sync.dma_start(out=tab[a][:].bitcast(I32), in_=tab_words[a].rearrange("p t i -> p (t i)").bitcast(I32))
@@ -73,67 +74,83 @@ def tile_list_carpool_pair_cards_kernel(
         def load_wb(a):
             nc.sync.dma_start(out=wb_raw[a][:], in_=wb[a * 512 : (a + 1) * 512, :].rearrange("(p j) c -> p j c", j=PACK))
 
+        day_rows = weekday.rearrange("(g t i) j -> t g i j", t=PACK, i=8)
+        wc_rows = wc.rearrange("(g t i) n -> t g i n", t=PACK, i=8)
+
+        def load_day(c):
+            for t in range(PACK):
+                nc.sync.dma_start(out=day[c][:, t, :], in_=day_rows[t][:, :, entries(c)])
+
         nc.sync.dma_start(riders[:], offs)
-        nc.sync.dma_start(out=w4_raw[:].bitcast(I32), in_=w4_words.bitcast(I32).rearrange("a p c -> p a c"))
+        nc.sync.dma_start(out=w4_raw[:], in_=w4_words.bitcast(I32).rearrange("a p c -> p a c"))
         scales_i32 = tab_scales.bitcast(I32)
         for q in range(QUADS):
             nc.sync.dma_start(
                 out=tab_planes[32 * q : 32 * q + 4 * PASSES, :].bitcast(I32), in_=scales_i32[:, 4 * q : 4 * q + 4, :]
             )
-        nc.sync.dma_start(drivers[:], offs2)
         load_tab(0)
+        load_wb(0)
+        nc.sync.dma_start(drivers[:], offs2)
         w4_scales_i32 = w4_scales.bitcast(I32)
         for q in range(QUADS):
             nc.sync.dma_start(
-                out=w4_raw_planes[32 * q : 32 * q + 4, :, :].bitcast(I32),
+                out=w4_raw_planes[32 * q : 32 * q + 4, :, :],
                 in_=w4_scales_i32[:, 4 * q : 4 * q + 4, :].rearrange("a r c -> r a c"),
             )
-        load_wb(0)
-        load_tab(1)
         load_wb(1)
-        day_rows = weekday.rearrange("(p t) j -> p t j", t=PACK)
-        wc_rows = wc.rearrange("(p t) n -> p t n", t=PACK)
-        nc.sync.dma_start(out=day[0][:], in_=day_rows[:, :, entries(0)])
-        nc.sync.dma_start(out=gains[:], in_=gain.rearrange("(p t) -> p t", t=PACK))
-        nc.sync.dma_start(out=wc_raw[0][:], in_=wc_rows[:, :, 0:WC_PIECE])
-        nc.sync.dma_start(out=day[1][:], in_=day_rows[:, :, entries(1)])
+        load_tab(1)
+        load_day(0)
+        gain_rows = gain.rearrange("(g t i o) -> t g i o", t=PACK, i=8, o=1)
+        for t in range(PACK):
+            with nc.allow_non_contiguous_dma("one gain value to a partition and slot"):
+                nc.sync.dma_start(out=gains[t][:], in_=gain_rows[t])
+            nc.sync.dma_start(out=wc_raw[:, t, :], in_=wc_rows[t])
+        load_day(1)
         nc.sync.dma_start(cards[:], offs3)
         with nc.allow_non_contiguous_dma("one rank value to a partition and row tile"):
             nc.sync.dma_start(out=ranks[:], in_=rank.rearrange("(u p) -> p u", p=P))
         nc.sync.dma_start(out=go[:], in_=wgo)
-        for i in range(1, N // WC_PIECE):
-            nc.sync.dma_start(out=wc_raw[i][:], in_=wc_rows[:, :, i * WC_PIECE : (i + 1) * WC_PIECE])
 
         rider_planes = held([P, S], U8, "rider_planes")
         driver_planes = held([P, S], U8, "driver_planes")
         nc.vector.tensor_copy(rider_planes[:], tab_planes[:].indirect(riders[:]))
-        for q in range(QUADS):
-            nc.scalar.dma_start(
-                out=rider_plane1[32 * q : 32 * q + 4, :].bitcast(I32),
-                in_=rider_planes[32 * q + 4 : 32 * q + 8, :].bitcast(I32),
-            )
+        nc.scalar.dma_start(out=rider_plane1[0:100, :].bitcast(I32), in_=rider_planes[4:104, :].bitcast(I32))
         nc.vector.tensor_copy(driver_planes[:], tab_planes[:].indirect(drivers[:]))
 
-        w4 = held([P, PASSES, PACK, P], U16, "w4")
-        w4_planes = held([P, PASSES, PACK, P], U8, "w4_planes")
-        nc.vector.tensor_copy(w4[:], w4_raw[:].rearrange("p a (m t) -> p a t m", t=PACK))
-        nc.vector.tensor_copy(w4_planes[:], w4_raw_planes[:].rearrange("p a (m t) -> p a t m", t=PACK))
+        w4 = held([P, PASSES, PACK, P // 2], I32, "w4")
+        w4_planes = held([P, PASSES, PACK, P // 4], I32, "w4_planes")
+        nc.vector.tensor_copy(
+            w4[:].rearrange("p a t (g w) -> p a t g w", w=4), w4_raw[:].rearrange("p a (g t w) -> p a t g w", t=PACK, w=4)
+        )
+        nc.vector.tensor_copy(
+            w4_planes[:].rearrange("p a t (g w) -> p a t g w", w=2),
+            w4_raw_planes[:].rearrange("p a (g t w) -> p a t g w", t=PACK, w=2),
+        )
 
         rider_words, driver_words = {}, {}
 
-        def gather_words(c, a):
-            rider_words[c, a] = held([P, CHUNK], U32, "rider_words%d%d" % (c, a))
-            driver_words[c, a] = held([P, CHUNK], U32, "driver_words%d%d" % (c, a))
-            nc.vector.tensor_copy(rider_words[c, a][:], tab[a][:].indirect(riders[:, list_columns(c)]))
-            nc.vector.tensor_copy(driver_words[c, a][:], tab[a][:].indirect(drivers[:, list_columns(c)]))
+        def gather_pass0():
+            words = held([P, 2, S], U32, "words0")
+            nc.vector.tensor_copy(words[:, 0, :], tab[0][:].indirect(riders[:]))
+            nc.vector.tensor_copy(words[:, 1, :], tab[0][:].indirect(drivers[:]))
+            for c in range(CHUNKS):
+                rider_words[c, 0] = words[:, 0, entries(c)]
+                driver_words[c, 0] = words[:, 1, entries(c)]
+
+        def gather_pass1(c, after=None):
+            words = held([P, 2, CHUNK], U32, "words1%d" % c, after)
+            rider_words[c, 1] = words[:, 0, :]
+            driver_words[c, 1] = words[:, 1, :]
+            nc.vector.tensor_copy(rider_words[c, 1], tab[1][:].indirect(riders[:, list_columns(c)]))
+            nc.vector.tensor_copy(driver_words[c, 1], tab[1][:].indirect(drivers[:, list_columns(c)]))
 
         wb_rounded, wb_codes, wb_planes = {}, {}, {}
 
         def round_wb(a):
             wb_rounded[a] = held([P, PACK, P, PACK], BF16, "wb_rounded%d" % a)
             nc.scalar.copy(
-                wb_rounded[a][:].rearrange("p t m j -> p m j t"),
-                wb_raw[a][:].rearrange("p j (m t) -> p m j t", t=PACK),
+                wb_rounded[a][:].rearrange("p t (g i) j -> p t g i j", i=8),
+                wb_raw[a][:].rearrange("p j (g t i) -> p t g i j", t=PACK, i=8),
             )
 
         def quantise_wb(a):
@@ -151,7 +168,7 @@ def tile_list_carpool_pair_cards_kernel(
             wc_rounded[i] = held([P, WC_PIECE, PACK], BF16, "wc_rounded%d" % i)
             nc.scalar.copy(
                 wc_rounded[i][:].rearrange("p (n i) t -> p n t i", i=4),
-                wc_raw[i][:].rearrange("p t (n i) -> p n t i", i=4),
+                wc_raw[:, :, i * WC_PIECE : (i + 1) * WC_PIECE].rearrange("p t (n i) -> p n t i", i=4),
             )
 
         def quantise_wc(i):
@@ -163,39 +180,42 @@ def tile_list_carpool_pair_cards_kernel(
                 in_=wc_rounded[i][:].rearrange("p n t -> p (n t)"),
             )
 
-        rider_sums, ra, db, z, z_rounded, z_codes, z_planes = {}, {}, {}, {}, {}, {}, {}
+        rider_sums, driver_sums, ra, db, z, z_rounded, z_codes, z_planes = {}, {}, {}, {}, {}, {}, {}, {}
 
-        def rider_products(c):
+        def rider_pass(c, a):
+            plane = rider_planes if a == 0 else rider_plane1
             for t in range(PACK):
-                rider_sums[c, t] = psum.tile([P, CHUNK], F32, name="bank")
-                for a in range(PASSES):
-                    plane = rider_planes if a == 0 else rider_plane1
-                    nc.tensor.matmul_mx(
-                        out=rider_sums[c, t][:],
-                        lhsT=w4[:, a, t, :].bitcast(FP4X4),
-                        lhsT_scale=w4_planes[:, a, t, :],
-                        rhs=rider_words[c, a][:].bitcast(FP8X4),
-                        rhs_scale=plane[:, entries(c)],
-                        start=(a == 0),
-                        stop=(a == PASSES - 1),
-                    )
+                if a == 0:
+                    rider_sums[c, t] = psum.tile([P, CHUNK], F32, name="bank")
+                nc.tensor.matmul_mx(
+                    out=rider_sums[c, t][:],
+                    lhsT=w4[:, a, t, :].bitcast(FP4X4),
+                    lhsT_scale=w4_planes[:, a, t, :].bitcast(U8),
+                    rhs=rider_words[c, a].bitcast(FP8X4),
+                    rhs_scale=plane[:, entries(c)],
+                    start=(a == 0),
+                    stop=(a == PASSES - 1),
+                )
+
+        def driver_pass(c, a):
+            for t in range(PACK):
+                if a == 0:
+                    driver_sums[c, t] = psum.tile([P, CHUNK], F32, name="bank")
+                columns = slice(t * P, (t + 1) * P)
+                nc.tensor.matmul_mx(
+                    out=driver_sums[c, t][:],
+                    lhsT=wb_codes[a][:, columns].bitcast(FP8X4),
+                    lhsT_scale=wb_planes[a][:, columns],
+                    rhs=driver_words[c, a].bitcast(FP8X4),
+                    rhs_scale=driver_planes[4 * a :, entries(c)],
+                    start=(a == 0),
+                    stop=(a == PASSES - 1),
+                )
 
         def driver_features(c):
+            db[c] = held([P, PACK, CHUNK], F32, "db%d" % c)
             for t in range(PACK):
-                bank = psum.tile([P, CHUNK], F32, name="bank")
-                columns = slice(t * P, (t + 1) * P)
-                for a in range(PASSES):
-                    nc.tensor.matmul_mx(
-                        out=bank[:],
-                        lhsT=wb_codes[a][:, columns].bitcast(FP8X4),
-                        lhsT_scale=wb_planes[a][:, columns],
-                        rhs=driver_words[c, a][:].bitcast(FP8X4),
-                        rhs_scale=driver_planes[4 * a :, entries(c)],
-                        start=(a == 0),
-                        stop=(a == PASSES - 1),
-                    )
-                db[c, t] = held([P, CHUNK], F32, "db%d%d" % (c, t))
-                nc.scalar.activation(db[c, t][:], bank[:], ACT.Sin)
+                nc.scalar.activation(db[c][:, t, :], driver_sums[c, t][:], ACT.Sin)
 
         def rider_features(c):
             for t in range(PACK):
@@ -207,7 +227,7 @@ def tile_list_carpool_pair_cards_kernel(
         def pair_features(c):
             z[c] = held([P, PACK, CHUNK], F32, "z%d" % c)
             for t in range(PACK):
-                nc.vector.scalar_tensor_tensor(z[c][:, t, :], ra[c, t][:], gains[:, t : t + 1], db[c, t][:], MULT, MULT)
+                nc.vector.scalar_tensor_tensor(z[c][:, t, :], ra[c, t][:], gains[t][:], db[c][:, t, :], MULT, MULT)
             z_rounded[c] = held([P, CHUNK, PACK], BF16, "z_rounded%d" % c)
             nc.scalar.copy(
                 z_rounded[c][:].rearrange("p (j i) t -> p j t i", i=4),
@@ -223,9 +243,13 @@ def tile_list_carpool_pair_cards_kernel(
                 in_=z_rounded[c][:].rearrange("p j t -> p (j t)"),
             )
 
-        y = [held([P, S], F32, "y%d" % u) for u in range(ROW_TILES)]
+        y, pages = {}, {}
 
-        def card_values(u, c):
+        def clear_page(i, after):
+            pages[i] = held([P, T], F32, "page%d" % i, after)
+            nc.gpsimd.memset(pages[i][:], 0.0)
+
+        def card_values(u, c, values):
             piece, first = divmod(u * P, WC_PIECE)
             columns = slice(first, first + P)
             bank = psum.tile([P, CHUNK], F32, name="bank")
@@ -238,54 +262,60 @@ def tile_list_carpool_pair_cards_kernel(
                 start=True,
                 stop=True,
             )
-            nc.scalar.activation(y[u][:, entries(c)], bank[:], ACT.Copy, scale=ranks[:, u : u + 1])
+            nc.scalar.activation(values, bank[:], ACT.Copy, scale=ranks[:, u : u + 1])
 
-        def place_chunk(u, c):
-            nc.vector.tensor_tensor(
-                pages[u % PAGES][:].indirect(cards[:, list_columns(c)]), y[u][:, entries(c)], go[:, entries(c)], MULT
-            )
+        def place_chunk(u, c, after=None):
+            values = held([P, CHUNK], F32, "y%d%d" % (u, c), after)
+            card_values(u, c, values[:])
+            nc.vector.tensor_tensor(pages[u][:].indirect(cards[:, list_columns(c)]), values[:], go[:, entries(c)], MULT)
 
         def place_all(u):
-            nc.vector.tensor_tensor(pages[u % PAGES][:].indirect(cards[:]), y[u][:], go[:], MULT)
+            values = held([P, S], F32, "y%d" % u)
+            for c in range(CHUNKS):
+                card_values(u, c, values[:, entries(c)])
+            nc.vector.tensor_tensor(pages[u % PAGES][:].indirect(cards[:]), values[:], go[:], MULT)
 
         def store(u):
             nc.sync.dma_start(out=out[u * P : (u + 1) * P, :], in_=pages[u % PAGES][:])
 
-        for a in range(PASSES):
-            gather_words(0, a)
-        rider_products(0)
-        for a in range(PASSES):
-            round_wb(a)
-            gather_words(1, a)
-            quantise_wb(a)
-        driver_features(0)
+        gather_pass0()
+        rider_pass(0, 0)
+        round_wb(0)
+        quantise_wb(0)
+        driver_pass(0, 0)
+        round_wb(1)
+        gather_pass1(0)
+        rider_pass(0, 1)
+        quantise_wb(1)
+        driver_pass(0, 1)
         rider_features(0)
-        round_wc(0)
+        driver_features(0)
+        gather_pass1(1, "day0")
+        clear_page(0, "tab1")
         pair_features(0)
-        rider_products(1)
-        driver_features(1)
-        rider_features(1)
+        clear_page(1, "db0")
+        round_wc(0)
+        rider_pass(1, 0)
+        rider_pass(1, 1)
         quantise_wc(0)
         quantise_z(0)
-        card_values(0, 0)
+        clear_page(2, "z_rounded0")
         place_chunk(0, 0)
+        rider_features(1)
+        driver_pass(1, 0)
+        driver_pass(1, 1)
+        driver_features(1)
         pair_features(1)
-        card_values(1, 0)
-        place_chunk(1, 0)
         round_wc(1)
         quantise_wc(1)
+        place_chunk(1, 0, "ra11")
         quantise_z(1)
-        card_values(2, 0)
-        place_chunk(2, 0)
+        place_chunk(2, 0, "z1")
+        round_wc(2)
+        quantise_wc(2)
         for u in range(PAGES):
-            card_values(u, 1)
             place_chunk(u, 1)
             store(u)
-            if u == 0:
-                round_wc(2)
-                quantise_wc(2)
         for u in range(PAGES, ROW_TILES):
-            for c in range(CHUNKS):
-                card_values(u, c)
             place_all(u)
             store(u)

@@ -107,9 +107,9 @@ def tile_list_carpool_pair_cards_kernel(
             nc.sync.dma_start(out=wc_raw[:, t, :], in_=wc_rows[t])
         load_day(1)
         nc.sync.dma_start(cards[:], offs3)
+        nc.sync.dma_start(out=go[:], in_=wgo)
         with nc.allow_non_contiguous_dma("one rank value to a partition and row tile"):
             nc.sync.dma_start(out=ranks[:], in_=rank.rearrange("(u p) -> p u", p=P))
-        nc.sync.dma_start(out=go[:], in_=wgo)
 
         rider_planes = held([P, S], U8, "rider_planes")
         driver_planes = held([P, S], U8, "driver_planes")
@@ -137,12 +137,15 @@ def tile_list_carpool_pair_cards_kernel(
                 rider_words[c, 0] = words[:, 0, entries(c)]
                 driver_words[c, 0] = words[:, 1, entries(c)]
 
-        def gather_pass1(c, after=None):
-            words = held([P, 2, CHUNK], U32, "words1%d" % c, after)
-            rider_words[c, 1] = words[:, 0, :]
-            driver_words[c, 1] = words[:, 1, :]
-            nc.vector.tensor_copy(rider_words[c, 1], tab[1][:].indirect(riders[:, list_columns(c)]))
-            nc.vector.tensor_copy(driver_words[c, 1], tab[1][:].indirect(drivers[:, list_columns(c)]))
+        def gather_riders1(c, after=None):
+            words = held([P, CHUNK], U32, "rider_words1%d" % c, after)
+            rider_words[c, 1] = words[:]
+            nc.vector.tensor_copy(words[:], tab[1][:].indirect(riders[:, list_columns(c)]))
+
+        def gather_drivers1(c, after=None):
+            words = held([P, CHUNK], U32, "driver_words1%d" % c, after)
+            driver_words[c, 1] = words[:]
+            nc.vector.tensor_copy(words[:], tab[1][:].indirect(drivers[:, list_columns(c)]))
 
         wb_rounded, wb_codes, wb_planes = {}, {}, {}
 
@@ -167,8 +170,8 @@ def tile_list_carpool_pair_cards_kernel(
         def round_wc(i):
             wc_rounded[i] = held([P, WC_PIECE, PACK], BF16, "wc_rounded%d" % i)
             nc.scalar.copy(
-                wc_rounded[i][:].rearrange("p (n i) t -> p n t i", i=4),
-                wc_raw[:, :, i * WC_PIECE : (i + 1) * WC_PIECE].rearrange("p t (n i) -> p n t i", i=4),
+                wc_rounded[i][:],
+                wc_raw[:, :, i * WC_PIECE : (i + 1) * WC_PIECE].rearrange("p t n -> p n t"),
             )
 
         def quantise_wc(i):
@@ -212,26 +215,23 @@ def tile_list_carpool_pair_cards_kernel(
                     stop=(a == PASSES - 1),
                 )
 
-        def driver_features(c):
+        def features(c):
             db[c] = held([P, PACK, CHUNK], F32, "db%d" % c)
-            for t in range(PACK):
-                nc.scalar.activation(db[c][:, t, :], driver_sums[c, t][:], ACT.Sin)
-
-        def rider_features(c):
             for t in range(PACK):
                 weighted = ring.tile([P, CHUNK], F32, name="weighted")
                 nc.vector.tensor_tensor(weighted[:], rider_sums[c, t][:], day[c][:, t, :], MULT)
                 ra[c, t] = held([P, CHUNK], F32, "ra%d%d" % (c, t))
                 nc.scalar.activation(ra[c, t][:], weighted[:], ACT.Tanh)
+                nc.scalar.activation(db[c][:, t, :], driver_sums[c, t][:], ACT.Sin)
 
         def pair_features(c):
-            z[c] = held([P, PACK, CHUNK], F32, "z%d" % c)
+            z[c] = held([P, PACK, CHUNK], BF16, "z%d" % c)
             for t in range(PACK):
                 nc.vector.scalar_tensor_tensor(z[c][:, t, :], ra[c, t][:], gains[t][:], db[c][:, t, :], MULT, MULT)
             z_rounded[c] = held([P, CHUNK, PACK], BF16, "z_rounded%d" % c)
             nc.scalar.copy(
-                z_rounded[c][:].rearrange("p (j i) t -> p j t i", i=4),
-                z[c][:].rearrange("p t (j i) -> p j t i", i=4),
+                z_rounded[c][:],
+                z[c][:].rearrange("p t j -> p j t"),
             )
 
         def quantise_z(c):
@@ -284,31 +284,31 @@ def tile_list_carpool_pair_cards_kernel(
         quantise_wb(0)
         driver_pass(0, 0)
         round_wb(1)
-        gather_pass1(0)
+        gather_riders1(0)
+        gather_drivers1(0)
         rider_pass(0, 1)
         quantise_wb(1)
+        clear_page(0, "wb_rounded1")
         driver_pass(0, 1)
-        rider_features(0)
-        driver_features(0)
-        gather_pass1(1, "day0")
-        clear_page(0, "tab1")
+        features(0)
+        gather_riders1(1, "day0")
         pair_features(0)
-        clear_page(1, "db0")
+        gather_drivers1(1, "ra02")
         round_wc(0)
         rider_pass(1, 0)
         rider_pass(1, 1)
         quantise_wc(0)
         quantise_z(0)
-        clear_page(2, "z_rounded0")
+        clear_page(1, "z_rounded0")
         place_chunk(0, 0)
-        rider_features(1)
+        clear_page(2, "y00")
         driver_pass(1, 0)
         driver_pass(1, 1)
-        driver_features(1)
+        features(1)
         pair_features(1)
+        place_chunk(1, 0, "ra11")
         round_wc(1)
         quantise_wc(1)
-        place_chunk(1, 0, "ra11")
         quantise_z(1)
         place_chunk(2, 0, "z1")
         round_wc(2)

@@ -18,11 +18,16 @@ ACT = mybir.ActivationFunctionType
 
 P = 128
 PACK = 4
-PASSES = K // (P * PACK)
+K_PASS = P * PACK
+PASSES = K // K_PASS
 QUADS = 4
+PLANE_ROWS = 4
+RUN = 8
+GROUP = 16
 CHUNK = 512
 CHUNKS = S // CHUNK
 ROW_TILES = N // P
+BANKS = 8
 PAGES = 3
 WC_PIECE = 256
 
@@ -33,8 +38,8 @@ def tile_list_carpool_pair_cards_kernel(
     nc = tc.nc
     with ExitStack() as ctx:
         keep = ctx.enter_context(tc.tile_pool(name="keep", bufs=1))
-        ring = ctx.enter_context(tc.tile_pool(name="ring", bufs=4))
-        psum = ctx.enter_context(tc.psum_pool(name="psum", bufs=8))
+        ring = ctx.enter_context(tc.tile_pool(name="ring", bufs=PACK))
+        psum = ctx.enter_context(tc.psum_pool(name="psum", bufs=BANKS))
 
         def held(shape, dtype, name, after=None):
             return keep.tile(shape, dtype, name=name, tag=after or name, align_bytes=64)
@@ -43,11 +48,11 @@ def tile_list_carpool_pair_cards_kernel(
             return slice(c * CHUNK, (c + 1) * CHUNK)
 
         def list_columns(c):
-            return slice(c * CHUNK // 16, (c + 1) * CHUNK // 16)
+            return slice(c * CHUNK // GROUP, (c + 1) * CHUNK // GROUP)
 
-        riders = held([P, S // 16], U16, "riders")
-        drivers = held([P, S // 16], U16, "drivers")
-        cards = held([P, S // 16], U16, "cards")
+        riders = held([P, S // GROUP], U16, "riders")
+        drivers = held([P, S // GROUP], U16, "drivers")
+        cards = held([P, S // GROUP], U16, "cards")
         tab_planes = held([P, T], U8, "tab_planes")
         tab = [held([P, T], U32, "tab%d" % a) for a in range(PASSES)]
         w4_raw = held([P, PASSES, H // 2], I32, "w4_raw")
@@ -68,14 +73,16 @@ def tile_list_carpool_pair_cards_kernel(
         nc.gpsimd.memset(warm_in[:], 0.0)
         nc.scalar.activation(warm_out[:], warm_in[:], ACT.Silu)
 
+        wb_rows = wb.rearrange("(a p j) r -> a p j r", a=PASSES, j=PACK)
+        day_rows = weekday.rearrange("(g t i) j -> t g i j", t=PACK, i=RUN)
+        wc_rows = wc.rearrange("(g t i) n -> t g i n", t=PACK, i=RUN)
+        gain_rows = gain.rearrange("(g t i o) -> t g i o", t=PACK, i=RUN, o=1)
+
         def load_tab(a):
             nc.sync.dma_start(out=tab[a][:].bitcast(I32), in_=tab_words[a].rearrange("p t i -> p (t i)").bitcast(I32))
 
         def load_wb(a):
-            nc.sync.dma_start(out=wb_raw[a][:], in_=wb[a * 512 : (a + 1) * 512, :].rearrange("(p j) c -> p j c", j=PACK))
-
-        day_rows = weekday.rearrange("(g t i) j -> t g i j", t=PACK, i=8)
-        wc_rows = wc.rearrange("(g t i) n -> t g i n", t=PACK, i=8)
+            nc.sync.dma_start(out=wb_raw[a][:], in_=wb_rows[a])
 
         def load_day(c):
             for t in range(PACK):
@@ -86,7 +93,8 @@ def tile_list_carpool_pair_cards_kernel(
         scales_i32 = tab_scales.bitcast(I32)
         for q in range(QUADS):
             nc.sync.dma_start(
-                out=tab_planes[32 * q : 32 * q + 4 * PASSES, :].bitcast(I32), in_=scales_i32[:, 4 * q : 4 * q + 4, :]
+                out=tab_planes[32 * q : 32 * q + PLANE_ROWS * PASSES, :].bitcast(I32),
+                in_=scales_i32[:, PLANE_ROWS * q : PLANE_ROWS * (q + 1), :],
             )
         load_tab(0)
         load_wb(0)
@@ -94,13 +102,12 @@ def tile_list_carpool_pair_cards_kernel(
         w4_scales_i32 = w4_scales.bitcast(I32)
         for q in range(QUADS):
             nc.sync.dma_start(
-                out=w4_raw_planes[32 * q : 32 * q + 4, :, :],
-                in_=w4_scales_i32[:, 4 * q : 4 * q + 4, :].rearrange("a r c -> r a c"),
+                out=w4_raw_planes[32 * q : 32 * q + PLANE_ROWS, :, :],
+                in_=w4_scales_i32[:, PLANE_ROWS * q : PLANE_ROWS * (q + 1), :].rearrange("a row c -> row a c"),
             )
         load_wb(1)
         load_tab(1)
         load_day(0)
-        gain_rows = gain.rearrange("(g t i o) -> t g i o", t=PACK, i=8, o=1)
         for t in range(PACK):
             with nc.allow_non_contiguous_dma("one gain value to a partition and slot"):
                 nc.sync.dma_start(out=gains[t][:], in_=gain_rows[t])
@@ -114,17 +121,21 @@ def tile_list_carpool_pair_cards_kernel(
         rider_planes = held([P, S], U8, "rider_planes")
         driver_planes = held([P, S], U8, "driver_planes")
         nc.vector.tensor_copy(rider_planes[:], tab_planes[:].indirect(riders[:]))
-        nc.scalar.dma_start(out=rider_plane1[0:100, :].bitcast(I32), in_=rider_planes[4:104, :].bitcast(I32))
+        span = 32 * (QUADS - 1) + PLANE_ROWS
+        nc.scalar.dma_start(
+            out=rider_plane1[0:span, :].bitcast(I32), in_=rider_planes[PLANE_ROWS : PLANE_ROWS + span, :].bitcast(I32)
+        )
         nc.vector.tensor_copy(driver_planes[:], tab_planes[:].indirect(drivers[:]))
 
         w4 = held([P, PASSES, PACK, P // 2], I32, "w4")
         w4_planes = held([P, PASSES, PACK, P // 4], I32, "w4_planes")
         nc.vector.tensor_copy(
-            w4[:].rearrange("p a t (g w) -> p a t g w", w=4), w4_raw[:].rearrange("p a (g t w) -> p a t g w", t=PACK, w=4)
+            w4[:].rearrange("p a t (g w) -> p a t g w", w=RUN // 2),
+            w4_raw[:].rearrange("p a (g t w) -> p a t g w", t=PACK, w=RUN // 2),
         )
         nc.vector.tensor_copy(
-            w4_planes[:].rearrange("p a t (g w) -> p a t g w", w=2),
-            w4_raw_planes[:].rearrange("p a (g t w) -> p a t g w", t=PACK, w=2),
+            w4_planes[:].rearrange("p a t (g w) -> p a t g w", w=RUN // 4),
+            w4_raw_planes[:].rearrange("p a (g t w) -> p a t g w", t=PACK, w=RUN // 4),
         )
 
         rider_words, driver_words = {}, {}
@@ -152,8 +163,8 @@ def tile_list_carpool_pair_cards_kernel(
         def round_wb(a):
             wb_rounded[a] = held([P, PACK, P, PACK], BF16, "wb_rounded%d" % a)
             nc.scalar.copy(
-                wb_rounded[a][:].rearrange("p t (g i) j -> p t g i j", i=8),
-                wb_raw[a][:].rearrange("p j (g t i) -> p t g i j", t=PACK, i=8),
+                wb_rounded[a][:].rearrange("p t (g i) j -> p t g i j", i=RUN),
+                wb_raw[a][:].rearrange("p j (g t i) -> p t g i j", t=PACK, i=RUN),
             )
 
         def quantise_wb(a):
@@ -167,23 +178,23 @@ def tile_list_carpool_pair_cards_kernel(
 
         wc_rounded, wc_codes, wc_planes = {}, {}, {}
 
-        def round_wc(i):
-            wc_rounded[i] = held([P, WC_PIECE, PACK], BF16, "wc_rounded%d" % i)
+        def round_wc(piece):
+            wc_rounded[piece] = held([P, WC_PIECE, PACK], BF16, "wc_rounded%d" % piece)
             nc.scalar.copy(
-                wc_rounded[i][:],
-                wc_raw[:, :, i * WC_PIECE : (i + 1) * WC_PIECE].rearrange("p t n -> p n t"),
+                wc_rounded[piece][:],
+                wc_raw[:, :, piece * WC_PIECE : (piece + 1) * WC_PIECE].rearrange("p t n -> p n t"),
             )
 
-        def quantise_wc(i):
-            wc_codes[i] = held([P, WC_PIECE], U32, "wc_codes%d" % i)
-            wc_planes[i] = held([P, WC_PIECE], U8, "wc_planes%d" % i)
+        def quantise_wc(piece):
+            wc_codes[piece] = held([P, WC_PIECE], U32, "wc_codes%d" % piece)
+            wc_planes[piece] = held([P, WC_PIECE], U8, "wc_planes%d" % piece)
             nc.vector.quantize_mx(
-                out=wc_codes[i][:].bitcast(FP8X4),
-                scales=wc_planes[i][:],
-                in_=wc_rounded[i][:].rearrange("p n t -> p (n t)"),
+                out=wc_codes[piece][:].bitcast(FP8X4),
+                scales=wc_planes[piece][:],
+                in_=wc_rounded[piece][:].rearrange("p n t -> p (n t)"),
             )
 
-        rider_sums, driver_sums, ra, db, z, z_rounded, z_codes, z_planes = {}, {}, {}, {}, {}, {}, {}, {}
+        rider_sums, driver_sums, ra, db, z, z_woven, z_codes, z_planes = {}, {}, {}, {}, {}, {}, {}, {}
 
         def rider_pass(c, a):
             plane = rider_planes if a == 0 else rider_plane1
@@ -210,7 +221,7 @@ def tile_list_carpool_pair_cards_kernel(
                     lhsT=wb_codes[a][:, columns].bitcast(FP8X4),
                     lhsT_scale=wb_planes[a][:, columns],
                     rhs=driver_words[c, a].bitcast(FP8X4),
-                    rhs_scale=driver_planes[4 * a :, entries(c)],
+                    rhs_scale=driver_planes[PLANE_ROWS * a :, entries(c)],
                     start=(a == 0),
                     stop=(a == PASSES - 1),
                 )
@@ -228,11 +239,8 @@ def tile_list_carpool_pair_cards_kernel(
             z[c] = held([P, PACK, CHUNK], BF16, "z%d" % c)
             for t in range(PACK):
                 nc.vector.scalar_tensor_tensor(z[c][:, t, :], ra[c, t][:], gains[t][:], db[c][:, t, :], MULT, MULT)
-            z_rounded[c] = held([P, CHUNK, PACK], BF16, "z_rounded%d" % c)
-            nc.scalar.copy(
-                z_rounded[c][:],
-                z[c][:].rearrange("p t j -> p j t"),
-            )
+            z_woven[c] = held([P, CHUNK, PACK], BF16, "z_woven%d" % c)
+            nc.scalar.copy(z_woven[c][:], z[c][:].rearrange("p t j -> p j t"))
 
         def quantise_z(c):
             z_codes[c] = held([P, CHUNK], U32, "z_codes%d" % c)
@@ -240,14 +248,14 @@ def tile_list_carpool_pair_cards_kernel(
             nc.vector.quantize_mx(
                 out=z_codes[c][:].bitcast(FP8X4),
                 scales=z_planes[c][:],
-                in_=z_rounded[c][:].rearrange("p j t -> p (j t)"),
+                in_=z_woven[c][:].rearrange("p j t -> p (j t)"),
             )
 
-        y, pages = {}, {}
+        pages = {}
 
-        def clear_page(i, after):
-            pages[i] = held([P, T], F32, "page%d" % i, after)
-            nc.gpsimd.memset(pages[i][:], 0.0)
+        def clear_page(page, after):
+            pages[page] = held([P, T], F32, "page%d" % page, after)
+            nc.gpsimd.memset(pages[page][:], 0.0)
 
         def card_values(u, c, values):
             piece, first = divmod(u * P, WC_PIECE)
@@ -293,13 +301,14 @@ def tile_list_carpool_pair_cards_kernel(
         features(0)
         gather_riders1(1, "day0")
         pair_features(0)
-        gather_drivers1(1, "ra02")
+        clear_page(1, "db0")
+
         round_wc(0)
         rider_pass(1, 0)
         rider_pass(1, 1)
         quantise_wc(0)
         quantise_z(0)
-        clear_page(1, "z_rounded0")
+        gather_drivers1(1, "z_woven0")
         place_chunk(0, 0)
         clear_page(2, "y00")
         driver_pass(1, 0)
@@ -313,6 +322,7 @@ def tile_list_carpool_pair_cards_kernel(
         place_chunk(2, 0, "z1")
         round_wc(2)
         quantise_wc(2)
+
         for u in range(PAGES):
             place_chunk(u, 1)
             store(u)

from contextlib import ExitStack

import concourse.mybir as mybir

K, H, N, T, S = 1024, 512, 768, 2048, 1024
FLOPS = 2 * K * H * S * 2 + 2 * H * N * S

F32 = mybir.dt.float32
BF16 = mybir.dt.bfloat16
I32 = mybir.dt.int32
U32 = mybir.dt.uint32
U16 = mybir.dt.uint16
U8 = mybir.dt.uint8
FP8X4 = mybir.dt.float8_e4m3fn_x4
FP4X4 = mybir.dt.float4_e2m1fn_x4
MULT = mybir.AluOpType.mult
ACT = mybir.ActivationFunctionType

P = 128
PACK = 4
K_PASS = P * PACK
PASSES = K // K_PASS
QUADS = 4
PLANE_ROWS = 4
RUN = 8
GROUP = 16
CHUNK = 512
CHUNKS = S // CHUNK
ROW_TILES = N // P
BANKS = 8
PAGES = 3
WC_PIECE = 256


def tile_list_carpool_pair_cards_kernel(
    tc, tab_words, tab_scales, offs, offs2, offs3, w4_words, w4_scales, wb, weekday, gain, wc, rank, wgo, out
):
    nc = tc.nc
    with ExitStack() as ctx:
        keep = ctx.enter_context(tc.tile_pool(name="keep", bufs=1))
        ring = ctx.enter_context(tc.tile_pool(name="ring", bufs=PACK))
        psum = ctx.enter_context(tc.psum_pool(name="psum", bufs=BANKS))

        def held(shape, dtype, name, after=None):
            return keep.tile(shape, dtype, name=name, tag=after or name, align_bytes=64)

        def entries(c):
            return slice(c * CHUNK, (c + 1) * CHUNK)

        def list_columns(c):
            return slice(c * CHUNK // GROUP, (c + 1) * CHUNK // GROUP)

        riders = held([P, S // GROUP], U16, "riders")
        drivers = held([P, S // GROUP], U16, "drivers")
        cards = held([P, S // GROUP], U16, "cards")
        tab_planes = held([P, T], U8, "tab_planes")
        tab = [held([P, T], U32, "tab%d" % a) for a in range(PASSES)]
        w4_raw = held([P, PASSES, H // 2], I32, "w4_raw")
        w4_raw_planes = held([P, PASSES, H // 4], I32, "w4_raw_planes")
        rider_plane1 = held([P, S], U8, "rider_plane1")
        wb_raw = [held([P, PACK, H], F32, "wb_raw%d" % a) for a in range(PASSES)]
        day = [held([P, PACK, CHUNK], F32, "day%d" % c) for c in range(CHUNKS)]
        wc_raw = held([P, PACK, N], F32, "wc_raw")
        gains = [held([P, 1], F32, "gain%d" % t) for t in range(PACK)]
        ranks = held([P, ROW_TILES], F32, "ranks")
        go = held([P, S], F32, "go")

        nc.vector.memset(tab_planes[:].bitcast(I32), 0)
        nc.vector.memset(w4_raw_planes[:], 0)
        nc.vector.memset(rider_plane1[:].bitcast(I32), 0)
        warm_in = held([P, 1], F32, "warm_in")
        warm_out = held([P, 1], F32, "warm_out")
        nc.gpsimd.memset(warm_in[:], 0.0)
        nc.scalar.activation(warm_out[:], warm_in[:], ACT.Silu)

        wb_rows = wb.rearrange("(a p j) r -> a p j r", a=PASSES, j=PACK)
        day_rows = weekday.rearrange("(g t i) j -> t g i j", t=PACK, i=RUN)
        wc_rows = wc.rearrange("(g t i) n -> t g i n", t=PACK, i=RUN)
        gain_rows = gain.rearrange("(g t i o) -> t g i o", t=PACK, i=RUN, o=1)

        def load_tab(a):
            nc.sync.dma_start(out=tab[a][:].bitcast(I32), in_=tab_words[a].rearrange("p t i -> p (t i)").bitcast(I32))

        def load_wb(a):
            nc.sync.dma_start(out=wb_raw[a][:], in_=wb_rows[a])

        def load_day(c):
            for t in range(PACK):
                nc.sync.dma_start(out=day[c][:, t, :], in_=day_rows[t][:, :, entries(c)])

        nc.sync.dma_start(riders[:], offs)
        nc.sync.dma_start(out=w4_raw[:], in_=w4_words.bitcast(I32).rearrange("a p c -> p a c"))
        scales_i32 = tab_scales.bitcast(I32)
        for q in range(QUADS):
            nc.sync.dma_start(
                out=tab_planes[32 * q : 32 * q + PLANE_ROWS * PASSES, :].bitcast(I32),
                in_=scales_i32[:, PLANE_ROWS * q : PLANE_ROWS * (q + 1), :],
            )
        load_tab(0)
        load_wb(0)
        nc.sync.dma_start(drivers[:], offs2)
        w4_scales_i32 = w4_scales.bitcast(I32)
        for q in range(QUADS):
            nc.sync.dma_start(
                out=w4_raw_planes[32 * q : 32 * q + PLANE_ROWS, :, :],
                in_=w4_scales_i32[:, PLANE_ROWS * q : PLANE_ROWS * (q + 1), :].rearrange("a row c -> row a c"),
            )
        load_wb(1)
        load_tab(1)
        load_day(0)
        for t in range(PACK):
            with nc.allow_non_contiguous_dma("one gain value to a partition and slot"):
                nc.sync.dma_start(out=gains[t][:], in_=gain_rows[t])
            nc.sync.dma_start(out=wc_raw[:, t, :], in_=wc_rows[t])
        load_day(1)
        nc.sync.dma_start(cards[:], offs3)
        nc.sync.dma_start(out=go[:], in_=wgo)
        with nc.allow_non_contiguous_dma("one rank value to a partition and row tile"):
            nc.sync.dma_start(out=ranks[:], in_=rank.rearrange("(u p) -> p u", p=P))

        rider_planes = held([P, S], U8, "rider_planes")
        driver_planes = held([P, S], U8, "driver_planes")
        nc.vector.tensor_copy(rider_planes[:], tab_planes[:].indirect(riders[:]))
        span = 32 * (QUADS - 1) + PLANE_ROWS
        nc.scalar.dma_start(
            out=rider_plane1[0:span, :].bitcast(I32), in_=rider_planes[PLANE_ROWS : PLANE_ROWS + span, :].bitcast(I32)
        )
        nc.vector.tensor_copy(driver_planes[:], tab_planes[:].indirect(drivers[:]))

        w4 = held([P, PASSES, PACK, P // 2], I32, "w4")
        w4_planes = held([P, PASSES, PACK, P // 4], I32, "w4_planes")
        nc.vector.tensor_copy(
            w4[:].rearrange("p a t (g w) -> p a t g w", w=RUN // 2),
            w4_raw[:].rearrange("p a (g t w) -> p a t g w", t=PACK, w=RUN // 2),
        )
        nc.vector.tensor_copy(
            w4_planes[:].rearrange("p a t (g w) -> p a t g w", w=RUN // 4),
            w4_raw_planes[:].rearrange("p a (g t w) -> p a t g w", t=PACK, w=RUN // 4),
        )

        rider_words, driver_words = {}, {}

        def gather_pass0():
            words = held([P, 2, S], U32, "words0")
            nc.vector.tensor_copy(words[:, 0, :], tab[0][:].indirect(riders[:]))
            nc.vector.tensor_copy(words[:, 1, :], tab[0][:].indirect(drivers[:]))
            for c in range(CHUNKS):
                rider_words[c, 0] = words[:, 0, entries(c)]
                driver_words[c, 0] = words[:, 1, entries(c)]

        def gather_riders1(c, after=None):
            words = held([P, CHUNK], U32, "rider_words1%d" % c, after)
            rider_words[c, 1] = words[:]
            nc.vector.tensor_copy(words[:], tab[1][:].indirect(riders[:, list_columns(c)]))

        def gather_drivers1(c, after=None):
            words = held([P, CHUNK], U32, "driver_words1%d" % c, after)
            driver_words[c, 1] = words[:]
            nc.vector.tensor_copy(words[:], tab[1][:].indirect(drivers[:, list_columns(c)]))

        wb_rounded, wb_codes, wb_planes = {}, {}, {}

        def round_wb(a):
            wb_rounded[a] = held([P, PACK, P, PACK], BF16, "wb_rounded%d" % a)
            nc.scalar.copy(
                wb_rounded[a][:].rearrange("p t (g i) j -> p t g i j", i=RUN),
                wb_raw[a][:].rearrange("p j (g t i) -> p t g i j", t=PACK, i=RUN),
            )

        def quantise_wb(a):
            wb_codes[a] = held([P, H], U32, "wb_codes%d" % a)
            wb_planes[a] = held([P, H], U8, "wb_planes%d" % a)
            nc.vector.quantize_mx(
                out=wb_codes[a][:].bitcast(FP8X4),
                scales=wb_planes[a][:],
                in_=wb_rounded[a][:].rearrange("p t m j -> p (t m j)"),
            )

        wc_rounded, wc_codes, wc_planes = {}, {}, {}

        def round_wc(piece):
            wc_rounded[piece] = held([P, WC_PIECE, PACK], BF16, "wc_rounded%d" % piece)
            nc.scalar.copy(
                wc_rounded[piece][:],
                wc_raw[:, :, piece * WC_PIECE : (piece + 1) * WC_PIECE].rearrange("p t n -> p n t"),
            )

        def quantise_wc(piece):
            wc_codes[piece] = held([P, WC_PIECE], U32, "wc_codes%d" % piece)
            wc_planes[piece] = held([P, WC_PIECE], U8, "wc_planes%d" % piece)
            nc.vector.quantize_mx(
                out=wc_codes[piece][:].bitcast(FP8X4),
                scales=wc_planes[piece][:],
                in_=wc_rounded[piece][:].rearrange("p n t -> p (n t)"),
            )

        rider_sums, driver_sums, ra, db, z, z_woven, z_codes, z_planes = {}, {}, {}, {}, {}, {}, {}, {}

        def rider_pass(c, a):
            plane = rider_planes if a == 0 else rider_plane1
            for t in range(PACK):
                if a == 0:
                    rider_sums[c, t] = psum.tile([P, CHUNK], F32, name="bank")
                nc.tensor.matmul_mx(
                    out=rider_sums[c, t][:],
                    lhsT=w4[:, a, t, :].bitcast(FP4X4),
                    lhsT_scale=w4_planes[:, a, t, :].bitcast(U8),
                    rhs=rider_words[c, a].bitcast(FP8X4),
                    rhs_scale=plane[:, entries(c)],
                    start=(a == 0),
                    stop=(a == PASSES - 1),
                )

        def driver_pass(c, a):
            for t in range(PACK):
                if a == 0:
                    driver_sums[c, t] = psum.tile([P, CHUNK], F32, name="bank")
                columns = slice(t * P, (t + 1) * P)
                nc.tensor.matmul_mx(
                    out=driver_sums[c, t][:],
                    lhsT=wb_codes[a][:, columns].bitcast(FP8X4),
                    lhsT_scale=wb_planes[a][:, columns],
                    rhs=driver_words[c, a].bitcast(FP8X4),
                    rhs_scale=driver_planes[PLANE_ROWS * a :, entries(c)],
                    start=(a == 0),
                    stop=(a == PASSES - 1),
                )

        def features(c):
            db[c] = held([P, PACK, CHUNK], F32, "db%d" % c)
            for t in range(PACK):
                weighted = ring.tile([P, CHUNK], F32, name="weighted")
                nc.vector.tensor_tensor(weighted[:], rider_sums[c, t][:], day[c][:, t, :], MULT)
                ra[c, t] = held([P, CHUNK], F32, "ra%d%d" % (c, t))
                nc.scalar.activation(ra[c, t][:], weighted[:], ACT.Tanh)
                nc.scalar.activation(db[c][:, t, :], driver_sums[c, t][:], ACT.Sin)

        def pair_features(c):
            z[c] = held([P, PACK, CHUNK], BF16, "z%d" % c)
            for t in range(PACK):
                nc.vector.scalar_tensor_tensor(z[c][:, t, :], ra[c, t][:], gains[t][:], db[c][:, t, :], MULT, MULT)
            z_woven[c] = held([P, CHUNK, PACK], BF16, "z_woven%d" % c)
            nc.scalar.copy(z_woven[c][:], z[c][:].rearrange("p t j -> p j t"))

        def quantise_z(c):
            z_codes[c] = held([P, CHUNK], U32, "z_codes%d" % c)
            z_planes[c] = held([P, CHUNK], U8, "z_planes%d" % c)
            nc.vector.quantize_mx(
                out=z_codes[c][:].bitcast(FP8X4),
                scales=z_planes[c][:],
                in_=z_woven[c][:].rearrange("p j t -> p (j t)"),
            )

        pages = {}

        def clear_page(page, after):
            pages[page] = held([P, T], F32, "page%d" % page, after)
            nc.gpsimd.memset(pages[page][:], 0.0)

        def card_values(u, c, values):
            piece, first = divmod(u * P, WC_PIECE)
            columns = slice(first, first + P)
            bank = psum.tile([P, CHUNK], F32, name="bank")
            nc.tensor.matmul_mx(
                out=bank[:],
                lhsT=wc_codes[piece][:, columns].bitcast(FP8X4),
                lhsT_scale=wc_planes[piece][:, columns],
                rhs=z_codes[c][:].bitcast(FP8X4),
                rhs_scale=z_planes[c][:],
                start=True,
                stop=True,
            )
            nc.scalar.activation(values, bank[:], ACT.Copy, scale=ranks[:, u : u + 1])

        def place_chunk(u, c, after=None):
            values = held([P, CHUNK], F32, "y%d%d" % (u, c), after)
            card_values(u, c, values[:])
            nc.vector.tensor_tensor(pages[u][:].indirect(cards[:, list_columns(c)]), values[:], go[:, entries(c)], MULT)

        def place_all(u):
            values = held([P, S], F32, "y%d" % u)
            for c in range(CHUNKS):
                card_values(u, c, values[:, entries(c)])
            nc.vector.tensor_tensor(pages[u % PAGES][:].indirect(cards[:]), values[:], go[:], MULT)

        def store(u):
            nc.sync.dma_start(out=out[u * P : (u + 1) * P, :], in_=pages[u % PAGES][:])

        gather_pass0()
        rider_pass(0, 0)
        round_wb(0)
        quantise_wb(0)
        driver_pass(0, 0)
        round_wb(1)
        gather_riders1(0)
        gather_drivers1(0)
        rider_pass(0, 1)
        quantise_wb(1)
        clear_page(0, "wb_rounded1")
        driver_pass(0, 1)
        features(0)
        gather_riders1(1, "day0")
        pair_features(0)
        clear_page(1, "db0")

        round_wc(0)
        rider_pass(1, 0)
        rider_pass(1, 1)
        quantise_wc(0)
        quantise_z(0)
        gather_drivers1(1, "z_woven0")
        place_chunk(0, 0)
        clear_page(2, "y00")
        driver_pass(1, 0)
        driver_pass(1, 1)
        features(1)
        pair_features(1)
        place_chunk(1, 0, "ra11")
        round_wc(1)
        quantise_wc(1)
        quantise_z(1)
        place_chunk(2, 0, "z1")
        round_wc(2)
        quantise_wc(2)

        for u in range(PAGES):
            place_chunk(u, 1)
            store(u)
        for u in range(PAGES, ROW_TILES):
            place_all(u)
            store(u)
